import numpy as np
import ml_dtypes


def mxq(x, axis, fmt="e4m3"):
    dtype, down = {"e4m3": (ml_dtypes.float8_e4m3fn, 7), "e5m2": (ml_dtypes.float8_e5m2, 14)}[fmt]
    v = np.moveaxis(np.asarray(x, np.float32).astype(ml_dtypes.bfloat16).astype(np.float64), axis, -1)
    blocks = v.reshape(v.shape[:-1] + (-1, 32))
    amax = np.abs(blocks).max(-1, keepdims=True)
    byte = np.maximum(np.where(amax > 0, np.frexp(amax)[1] - 1 + 127, 0) - down, 1)
    scale = np.exp2(byte - 127.0)
    codes = (blocks / scale).astype(np.float32).astype(dtype).astype(np.float64)
    return np.moveaxis((codes * scale).reshape(v.shape), -1, axis)


WIDE = False


def mx_kscale(k):
    if not WIDE:
        return np.ones(k)
    levels = np.array([10, -10, 5, -5, 0])
    if k % 512:
        return np.exp2(np.random.permutation(np.resize(levels, k // 32))).repeat(32)
    a = np.empty((k // 512, 16))
    for p in range(k // 512):
        a[p, :8] = np.random.permutation(np.resize(levels, 8))
        for g in range(8):
            far = levels[np.abs(levels - a[p, g]) >= 10]
            a[p, g + 8] = far[np.random.randint(len(far))]
    return np.exp2(a.ravel()).repeat(32)


def f64(x):
    return np.asarray(x).astype(np.float64)


def striped(idx):
    return np.tile(idx.reshape(-1, 16).T, (8, 1)).astype(np.uint16)


def unstriped(offs):
    return offs[:16].T.reshape(-1).astype(np.int64)


def striped8(idx):
    return np.concatenate([x.reshape(-1, 16).T for x in idx]).astype(np.uint16)


def runs(offs, k):
    lists = np.stack([offs[16 * r : 16 * r + 16].T.reshape(-1) for r in range(8)]).astype(np.int64)
    return lists[np.arange(k) % 512 // 64]


def pack_weight(w):
    k, n = w.shape
    w = f64(np.asarray(w, np.float32).astype(ml_dtypes.bfloat16)).reshape(k // 32, 32, n)
    amax = np.abs(w).max(1)
    byte = np.clip(np.where(amax > 0, np.frexp(amax)[1] - 1 + 127 - 7, 1), 1, 254)
    scaled = (w * np.exp2(127.0 - byte)[:, None, :]).reshape(k, n).astype(np.float32)
    words = np.ascontiguousarray(scaled.reshape(k // 512, 128, 4, n).transpose(0, 1, 3, 2)).astype(ml_dtypes.float8_e4m3fn).view(np.uint8)
    return words, np.ascontiguousarray(byte.astype(np.uint8).reshape(k // 512, 16, n))


def unpack_weight(words, scales):
    g, p, n, _ = words.shape
    vals = np.ascontiguousarray(words).view(ml_dtypes.float8_e4m3fn).astype(np.float64) * np.repeat(np.exp2(scales.astype(np.float64) - 127.0), 8, axis=1)[..., None]
    return vals.transpose(0, 1, 3, 2).reshape(g * 512, n)


K, T, S, H, G, U = 512, 1024, 256, 512, 2048, 512


def setup_inputs():
    n = np.random.standard_normal
    s = mx_kscale(K)[:, None]
    packed_xT = pack_weight(n((K, T)) * s)
    packed_dT = pack_weight(n((K, G)) / s)
    perm = np.random.permutation(U)
    return {
        "x_words": packed_xT[0],
        "x_scales": packed_xT[1],
        "w1": (n((K, H)) / np.sqrt(2 * K) / s).astype(np.float32),
        "w2": (n((K, H)) / np.sqrt(2 * K) / s).astype(np.float32),
        "gs": (np.random.uniform(0.5, 1.5, (K, 1)) * s).astype(np.float32),
        "d_words": packed_dT[0],
        "d_scales": packed_dT[1],
        "offs": striped8(np.random.randint(0, T, (8, S))),
        "hz": striped8(np.random.randint(0, T, (8, S))),
        "n1": striped(np.random.permutation(S)),
        "n2": striped(np.random.permutation(S)),
        "ka": striped8(np.random.randint(0, G, (8, H))),
        "kb": striped8(np.random.randint(0, G, (8, H))),
        "n3": striped(perm[:S]),
        "n4": striped(perm[S:]),
        "n5": striped(np.random.permutation(S)),
        "n6": striped(np.random.permutation(S)),
    }


def reference(x_words, x_scales, w1, w2, gs, d_words, d_scales, offs, hz, n1, n2, ka, kb, n3, n4, n5, n6):
    d_ka = unpack_weight(d_words, d_scales)[np.arange(K)[:, None], runs(ka, K)]
    xq = unpack_weight(x_words, x_scales)[np.arange(K)[:, None], runs(offs, K)]
    x_hz = unpack_weight(x_words, x_scales)[np.arange(K)[:, None], runs(hz, K)]
    y = mxq(f64(w1), 0, "e4m3").T @ xq + mxq(f64(w2), 0, "e4m3").T @ x_hz
    ds = np.zeros((H, S))
    ds[:, unstriped(n1)] = y
    z = f64(gs) * (np.maximum(y, ds[:, unstriped(n2)]))
    zq = mxq(z, 0, "e4m3")
    d_kb = unpack_weight(d_words, d_scales)[np.arange(K)[:, None], runs(kb, K)]
    h2 = 0.0625 * (d_ka.T @ zq + d_kb.T @ zq)
    st = h2 - h2[:, unstriped(n5)]
    up = np.maximum(st, st[:, unstriped(n6)])
    ph = np.zeros((H, U))
    ph[:, unstriped(n3)] = st
    out = ph.copy()
    out[:, unstriped(n4)] = up
    return out

from contextlib import ExitStack

import concourse.mybir as mybir

K, T, S, H, G, U = 512, 1024, 256, 512, 2048, 512
FLOPS = 2 * 2 * K * H * S + 2 * 2 * H * H * S

F32 = mybir.dt.float32
BF16 = mybir.dt.bfloat16
I32 = mybir.dt.int32
U32 = mybir.dt.uint32
U16 = mybir.dt.uint16
U8 = mybir.dt.uint8
FP8X4 = mybir.dt.float8_e4m3fn_x4
COPY = mybir.ActivationFunctionType.Copy
MAX = mybir.AluOpType.max
MULT = mybir.AluOpType.mult
SUB = mybir.AluOpType.subtract

P = 128
PACK = 4
HALF = S // 2
DS_COLS = 352
ROW_COLS = 272
W1_SCALAR = 48


def tile_picked_dhhzarelaypagew_none_p_kernel(tc, x_words, x_scales, w1, w2, gs, d_words, d_scales, offs, hz, n1, n2, ka, kb, n3, n4, n5, n6, out):
    nc = tc.nc
    with ExitStack() as ctx:
        pool = ctx.enter_context(tc.tile_pool(name="held", bufs=1))
        psum = ctx.enter_context(tc.psum_pool(name="psum", bufs=1))

        def sb(name, shape, dtype, tag=""):
            return pool.tile(shape, dtype, name=name, tag=tag or name, align_bytes=64)

        def load_list(name, src):
            tile = sb(name, [P, src.shape[1]], U16)
            nc.sync.dma_start(tile[:], src)
            return tile

        def load_scale_rows(name, src, width, tag=""):
            tile = sb(name, [P, width], U8, tag)
            nc.vector.memset(tile[:].bitcast(I32), 0)
            for e in range(2):
                nc.sync.dma_start(tile[e:P:16, :].bitcast(I32), src[0, e:16:2, :].bitcast(I32))
            return tile

        def load_words(name, src, width, tag=""):
            tile = sb(name, [P, width], U32, tag)
            nc.sync.dma_start(tile[:].bitcast(I32), src[0].rearrange("p n t -> p (n t)").bitcast(I32))
            return tile

        def load_weight(name, src, c0, c1):
            tile = sb(name, [P, PACK, c1 - c0], F32)
            nc.sync.dma_start(tile[:], src.rearrange("(p j) c -> p j c", j=PACK)[:, :, c0:c1])
            return tile

        def gather_pair(name, window, lists, n, dtype, tag=""):
            tile = sb(name, [P, 2 * n], dtype, tag)
            for u, offsets in enumerate(lists):
                nc.vector.tensor_copy(tile[:, u * n : (u + 1) * n], window[:].indirect(offsets[:]))
            return tile

        def place_scale_rows(name, picked, width, queue):
            plane = sb(name, [P, width], U8)
            nc.vector.tensor_copy(plane[:].bitcast(I32), picked[:].bitcast(I32))
            for e in range(2):
                queue.dma_start(plane[2 + e : P : 32, :].bitcast(I32), picked[16 + e : P : 32, :].bitcast(I32))
            return plane

        def deal(copy, grouped, raw, raw_m0, m0, m1):
            copy(
                grouped[:, :, m0:m1, :].rearrange("p t m j -> p m t j"),
                raw[:, :, PACK * (m0 - raw_m0) : PACK * (m1 - raw_m0)].rearrange("p j (m t) -> p m t j", t=PACK),
            )

        offs_t = load_list("offs_t", offs)
        hz_t = load_list("hz_t", hz)
        n1_t = load_list("n1_t", n1)
        n2_t = load_list("n2_t", n2)
        xs_rows = load_scale_rows("xs_rows", x_scales, T)
        xw = load_words("xw", x_words, T)
        w1_raw = load_weight("w1_raw", w1, 0, H)
        ka_t = load_list("ka_t", ka)
        kb_t = load_list("kb_t", kb)
        gs_t = sb("gs_t", [P, PACK], F32)
        nc.sync.dma_start(gs_t[:], gs.rearrange("(p t) o -> p (t o)", t=PACK))
        w2_raw = [load_weight("w2_raw%d" % h, w2, h * H // 2, (h + 1) * H // 2) for h in range(2)]
        n5_t = load_list("n5_t", n5)
        n6_t = load_list("n6_t", n6)
        n3_t = load_list("n3_t", n3)
        n4_t = load_list("n4_t", n4)

        ds = [sb("ds%d" % t, [P, DS_COLS], F32) for t in range(PACK)]
        h2 = [sb("h2_%d" % i, [P, ROW_COLS], F32) for i in range(PACK)]
        st = [sb("st%d" % i, [P, ROW_COLS], F32) for i in range(PACK)]
        for t in range(PACK):
            nc.vector.memset(ds[t][:, S:], 0.0)
            for tile in (h2[t], st[t]):
                nc.scalar.activation(tile[:, S:], ds[t][:, S:ROW_COLS], COPY)

        xs_picked = gather_pair("xs_picked", xs_rows, (offs_t, hz_t), S, U8)
        x_plane = place_scale_rows("x_plane", xs_picked, 2 * S, nc.scalar)
        x_codes = gather_pair("x_codes", xw, (offs_t, hz_t), S, U32)

        w_grouped = [sb("w_grouped%d" % u, [P, PACK, P, PACK], BF16) for u in range(2)]
        w_codes = [sb("w_codes%d" % u, [P, H], U32) for u in range(2)]
        w_plane = [sb("w_plane%d" % u, [P, H], U8) for u in range(2)]
        deal(nc.scalar.copy, w_grouped[0], w1_raw, 0, 0, W1_SCALAR)
        deal(nc.vector.tensor_copy, w_grouped[0], w1_raw, 0, W1_SCALAR, P)
        nc.vector.quantize_mx(w_codes[0][:].bitcast(FP8X4), w_plane[0][:], w_grouped[0][:].rearrange("p t m j -> p (t m j)"))
        deal(nc.scalar.copy, w_grouped[1], w2_raw[0], 0, 0, P // 2)
        deal(nc.vector.tensor_copy, w_grouped[1], w2_raw[1], P // 2, P // 2, P)

        y_ps = [psum.tile([P, S], F32, name="y_ps%d" % t) for t in range(PACK)]

        def first_pass(u, t):
            cols = slice(t * P, (t + 1) * P)
            picked = slice(u * S, (u + 1) * S)
            nc.tensor.matmul_mx(
                out=y_ps[t][:],
                lhsT=w_codes[u][:, cols].bitcast(FP8X4),
                lhsT_scale=w_plane[u][:, cols],
                rhs=x_codes[:, picked].bitcast(FP8X4),
                rhs_scale=x_plane[:, picked],
                start=(u == 0),
                stop=(u == 1),
            )

        y = [sb("y%d" % t, [P, S], F32) for t in range(PACK)]
        for t in range(PACK):
            cols = slice(t * P, (t + 1) * P)
            nc.vector.quantize_mx(w_codes[1][:, cols].bitcast(FP8X4), w_plane[1][:, cols], w_grouped[1][:, t, :, :].rearrange("p m j -> p (m j)"))
            first_pass(0, t)
            first_pass(1, t)
        nc.scalar.copy(y[0][:], y_ps[0][:])
        for t in range(1, PACK):
            nc.vector.tensor_copy(y[t][:], y_ps[t][:])

        dsc_rows = load_scale_rows("dsc_rows", d_scales, G, "xw")
        dw = load_words("dw", d_words, G, "w1_raw")
        dsc_picked = gather_pair("dsc_picked", dsc_rows, (ka_t, kb_t), H, U8, "w_grouped1")
        d_plane = place_scale_rows("d_plane", dsc_picked, 2 * H, nc.sync)
        d_codes = gather_pair("d_codes", dw, (ka_t, kb_t), H, U32)

        page = [sb("page%d" % i, [P, U], F32) for i in range(PACK)]
        fetched = [[sb("fetched%d_%d" % (half, t), [P, HALF], F32) for t in range(PACK)] for half in range(2)]
        larger = sb("larger", [P, 2, PACK, HALF], F32, "w1_raw")

        def send(t):
            nc.scalar.activation(ds[t][:].indirect(n1_t[:]), y[t][:], COPY)

        def fetch(half, t):
            nc.scalar.activation(fetched[half][t][:], ds[t][:].indirect(n2_t[:, half * HALF // 16 : (half + 1) * HALF // 16]), COPY)
            nc.vector.tensor_tensor(larger[:, half, t, :], fetched[half][t][:], y[t][:, half * HALF : (half + 1) * HALF], MAX)

        h2_first = psum.tile([P, PACK, HALF], F32, name="h2_first")
        h2_second = [psum.tile([P, HALF], F32, name="h2_second%d" % b) for b in range(2)]
        h2_rest = psum.tile([P, 2, HALF], F32, name="h2_rest")
        h2_ps = [[h2_first[:, i, :] for i in range(PACK)], [h2_second[0][:], h2_second[1][:], h2_rest[:, 0, :], h2_rest[:, 1, :]]]

        def second_product(half):
            z = sb("z%d" % half, [P, HALF, PACK], BF16)
            nc.vector.tensor_tensor(
                z[:].rearrange("p (c i) t -> p c t i", i=4),
                larger[:, half, :, :].rearrange("p t (c i) -> p c t i", i=4),
                gs_t[:].unsqueeze(1).unsqueeze(3).to_broadcast([P, HALF // 4, PACK, 4]),
                MULT,
            )
            z_codes = sb("z_codes%d" % half, [P, HALF], U32)
            z_plane = sb("z_plane%d" % half, [P, HALF], U8)
            nc.vector.quantize_mx(z_codes[:].bitcast(FP8X4), z_plane[:], z[:].rearrange("p c t -> p (c t)"))
            for i in range(PACK):
                for u in range(2):
                    cols = slice(u * H + i * P, u * H + (i + 1) * P)
                    nc.tensor.matmul_mx(
                        out=h2_ps[half][i],
                        lhsT=d_codes[:, cols].bitcast(FP8X4),
                        lhsT_scale=d_plane[:, cols],
                        rhs=z_codes[:].bitcast(FP8X4),
                        rhs_scale=z_plane[:],
                        start=(u == 0),
                        stop=(u == 1),
                    )
            for i in range(PACK):
                dst = h2[i][:, half * HALF : (half + 1) * HALF]
                if half == 1 and i == 0:
                    nc.scalar.activation(dst, h2_ps[half][i], COPY, scale=0.0625)
                else:
                    nc.vector.tensor_scalar(dst, h2_ps[half][i], 0.0625, None, MULT)

        send(0)
        for t in range(1, PACK):
            send(t)
            fetch(0, t - 1)
        fetch(0, PACK - 1)
        second_product(0)
        for t in range(PACK):
            fetch(1, t)
        second_product(1)

        other = [sb("other%d" % i, [P, S], F32) for i in range(PACK)]
        beside = [sb("beside%d" % i, [P, S], F32) for i in range(PACK)]
        up = [sb("up%d" % i, [P, S], F32) for i in range(PACK)]

        def step(i):
            nc.scalar.activation(other[i][:], h2[i][:].indirect(n5_t[:]), COPY)
            nc.vector.tensor_tensor(st[i][:, 0:S], h2[i][:, 0:S], other[i][:], SUB)

        def compare(i):
            nc.scalar.activation(beside[i][:], st[i][:].indirect(n6_t[:]), COPY)
            nc.vector.tensor_tensor(up[i][:], st[i][:, 0:S], beside[i][:], MAX)
            nc.scalar.activation(page[i][:].indirect(n3_t[:]), st[i][:, 0:S], COPY)

        def finish(i):
            nc.scalar.activation(page[i][:].indirect(n4_t[:]), up[i][:], COPY)
            nc.sync.dma_start(out[i * P : (i + 1) * P, :], page[i][:])

        step(0)
        step(1)
        for i in range(PACK):
            compare(i)
            if i + 2 < PACK:
                step(i + 2)
            finish(i)
